import numpy as np
import ml_dtypes


def mxq(x, axis, fmt="e4m3"):
    dtype, down = {"e4m3": (ml_dtypes.float8_e4m3fn, 7), "e5m2": (ml_dtypes.float8_e5m2, 14)}[fmt]
    v = np.moveaxis(np.asarray(x, np.float32).astype(ml_dtypes.bfloat16).astype(np.float64), axis, -1)
    blocks = v.reshape(v.shape[:-1] + (-1, 32))
    amax = np.abs(blocks).max(-1, keepdims=True)
    byte = np.maximum(np.where(amax > 0, np.frexp(amax)[1] - 1 + 127, 0) - down, 1)
    scale = np.exp2(byte - 127.0)
    codes = (blocks / scale).astype(np.float32).astype(dtype).astype(np.float64)
    return np.moveaxis((codes * scale).reshape(v.shape), -1, axis)


WIDE = False


def mx_kscale(k):
    if not WIDE:
        return np.ones(k)
    levels = np.array([10, -10, 5, -5, 0])
    if k % 512:
        return np.exp2(np.random.permutation(np.resize(levels, k // 32))).repeat(32)
    a = np.empty((k // 512, 16))
    for p in range(k // 512):
        a[p, :8] = np.random.permutation(np.resize(levels, 8))
        for g in range(8):
            far = levels[np.abs(levels - a[p, g]) >= 10]
            a[p, g + 8] = far[np.random.randint(len(far))]
    return np.exp2(a.ravel()).repeat(32)


def f64(x):
    return np.asarray(x).astype(np.float64)


def striped(idx):
    return np.tile(np.asarray(idx).reshape(-1, 16).T, (8, 1)).astype(np.uint16)


def unstriped(offs):
    return offs[:16].T.reshape(-1).astype(np.int64)


def striped8(idx):
    return np.asarray(idx).reshape(8, -1, 16).transpose(0, 2, 1).reshape(128, -1).astype(np.uint16)


def unstriped8(offs):
    return offs.reshape(8, 16, -1).transpose(0, 2, 1).reshape(8, -1).astype(np.int64)


def pick8(x, idx, run):
    r = np.arange(len(x))
    return x[r[:, None], idx[r % (8 * run) // run]]


E2M1 = np.array([0.0, 0.5, 1.0, 1.5, 2.0, 3.0, 4.0, 6.0, -0.0, -0.5, -1.0, -1.5, -2.0, -3.0, -4.0, -6.0])


def pack_weight(w, fmt):
    k, n = w.shape
    w = f64(np.asarray(w, np.float32).astype(ml_dtypes.bfloat16)).reshape(k // 32, 32, n)
    amax = np.abs(w).max(1)
    if fmt == "e4m3":
        byte = np.frexp(amax)[1] - 1 + 127 - 7
    else:
        mant, ex = np.frexp(amax / 6.0)
        byte = np.where(mant > 0.5, ex, ex - 1) + 127
    byte = np.clip(np.where(amax > 0, byte, 1), 1, 254)
    scaled = (w * np.exp2(127.0 - byte)[:, None, :]).reshape(k, n).astype(np.float32)
    by_word = np.ascontiguousarray(scaled.reshape(k // 512, 128, 4, n).transpose(0, 1, 3, 2))
    if fmt == "e4m3":
        words = by_word.astype(ml_dtypes.float8_e4m3fn).view(np.uint8)
    else:
        c = by_word.astype(ml_dtypes.float4_e2m1fn).view(np.uint8) & 0xF
        words = (c[..., 0::2] | (c[..., 1::2] << 4)).reshape(k // 512, 128, 2 * n)
    return np.ascontiguousarray(words), np.ascontiguousarray(byte.astype(np.uint8).reshape(k // 512, 16, n))


def unpack_weight(words, scales, fmt):
    g, _, n = scales.shape
    words = np.ascontiguousarray(words).reshape(g, 128, n, -1)
    if fmt == "e4m3":
        vals = words.view(ml_dtypes.float8_e4m3fn).astype(np.float64)
    else:
        nib = np.empty((g, 128, n, 4), np.uint8)
        nib[..., 0::2] = words & 0xF
        nib[..., 1::2] = words >> 4
        vals = E2M1[nib]
    vals = vals * np.repeat(np.exp2(scales.astype(np.float64) - 127.0), 8, axis=1)[..., None]
    return vals.transpose(0, 1, 3, 2).reshape(g * 512, n)


def sigmoid(v):
    return 1.0 / (1.0 + np.exp(-v))


K, R, F, T, J, U, M = 512, 128, 512, 2048, 512, 1024, 256


def setup_inputs():
    n = np.random.standard_normal
    idx = np.random.permutation(T)[:J]
    idx2 = np.random.permutation(U)[:J]
    idx3 = np.stack([np.random.permutation(J)[:M] for _ in range(8)])
    fk = mx_kscale(K)
    ff = mx_kscale(F)
    tabp = pack_weight(n((K, T)) / fk[:, None], "e2m1")
    dtabp = pack_weight(n((K, T)) / fk[:, None], "e2m1")
    return {
        "tab_words": tabp[0],
        "tab_scales": tabp[1],
        "w1": (n((K, R)) * 1 / np.sqrt(K) * fk[:, None]).astype(np.float32),
        "lift": (n((R, U)) * 0.5).astype(np.float32),
        "wo": (n((F, R)) * 1 / np.sqrt(F) * ff[:, None]).astype(np.float32),
        "dy": (n((F, M)) / ff[:, None]).astype(np.float32),
        "dtab_words": dtabp[0],
        "dtab_scales": dtabp[1],
        "og": (np.random.uniform(0.7, 2.0, (R, 1))).astype(np.float32),
        "base": (0.3 * n((R, J))).astype(np.float32),
        "offs": striped(idx),
        "offs2": striped(idx2),
        "offs3": striped8(idx3),
    }


def reference(tab_words, tab_scales, w1, lift, wo, dy, dtab_words, dtab_scales, og, base, offs, offs2, offs3):
    idx = unstriped(offs)
    idx2 = unstriped(offs2)
    idx3 = unstriped8(offs3)
    tabu = unpack_weight(tab_words, tab_scales, "e2m1")
    dtabu = unpack_weight(dtab_words, dtab_scales, "e2m1")
    w1q = mxq(f64(w1), 0, "e4m3")
    tabidxg = tabu[:, idx]
    a = w1q.T @ tabidxg
    dtabidxg = dtabu[:, idx]
    ta = w1q.T @ dtabidxg
    h1 = np.tanh(a)
    h2 = h1 * np.exp(f64(lift)[:, idx2])
    woq = mxq(f64(wo), 0, "e4m3")
    dyq = mxq(f64(dy), 0, "e4m3")
    c0 = woq.T @ dyq
    e1 = c0 * sigmoid(pick8(h2, idx3, 16)) * (1.0 + pick8(h2, idx3, 16) * (1.0 - sigmoid(pick8(h2, idx3, 16))))
    s1 = np.zeros((R, J))
    s1[np.arange(R)[:, None], idx3[np.arange(R) % 128 // 16]] = e1
    dh1 = s1 * np.exp(f64(lift)[:, idx2])
    xh1 = ta * (1.0 - np.square(h1))
    xh2 = xh1 * np.exp(f64(lift)[:, idx2])
    xe1 = (pick8(xh2, idx3, 16) * sigmoid(pick8(h2, idx3, 16)) * (1.0 - sigmoid(pick8(h2, idx3, 16))) * (1.0 + pick8(h2, idx3, 16) * (1.0 - sigmoid(pick8(h2, idx3, 16)))) + (pick8(xh2, idx3, 16) * (1.0 - sigmoid(pick8(h2, idx3, 16))) + pick8(xh2, idx3, 16) * sigmoid(pick8(h2, idx3, 16)) * (1.0 - sigmoid(pick8(h2, idx3, 16))) * (-1.0) * pick8(h2, idx3, 16)) * sigmoid(pick8(h2, idx3, 16))) * c0
    xs1 = np.zeros((R, J))
    xs1[np.arange(R)[:, None], idx3[np.arange(R) % 128 // 16]] = xe1
    xdh1 = xs1 * np.exp(f64(lift)[:, idx2])
    xda = xdh1 * (1.0 - np.square(h1)) + xh1 * h1 * 2.0 * (-1.0) * dh1
    y = xda * f64(og) + f64(base)
    return y

@@ -1,0 +1,174 @@
+from contextlib import ExitStack
+
+import concourse.mybir as mybir
+
+K, R, F, T, J, U, M = 512, 128, 512, 2048, 512, 1024, 256
+FLOPS = 2 * R * (2 * K * J + F * M)
+
+F32 = mybir.dt.float32
+BF16 = mybir.dt.bfloat16
+I32 = mybir.dt.int32
+U32 = mybir.dt.uint32
+U16 = mybir.dt.uint16
+U8 = mybir.dt.uint8
+FP8X4 = mybir.dt.float8_e4m3fn_x4
+FP4X4 = mybir.dt.float4_e2m1fn_x4
+ACT = mybir.ActivationFunctionType
+MULT = mybir.AluOpType.mult
+ADD = mybir.AluOpType.add
+SUB = mybir.AluOpType.subtract
+
+P = 128
+PACK = 4
+LIFT_WINDOW = 2048
+
+
+def tile_attend_hvliftedpicks_kernel(tc, tab_words, tab_scales, w1, lift, wo, dy, dtab_words, dtab_scales, og, base,
+                                      offs, offs2, offs3, out):
+    nc = tc.nc
+    with ExitStack() as ctx:
+        sb = ctx.enter_context(tc.tile_pool(name="sb", bufs=1))
+        ps = ctx.enter_context(tc.psum_pool(name="ps", bufs=1))
+
+        def t(name, cols, dtype=F32, tag=None):
+            return sb.tile([P, cols], dtype, name=name, tag=tag or name, align_bytes=64)
+
+        slots = t("slots", J // 16, U16)
+        lifts = t("lifts", J // 16, U16)
+        picks = t("picks", M // 16, U16)
+        tw = t("tw", T, U16)
+        tsc = t("tsc", T, U8)
+        dw = t("dw", T, U16)
+        dsc = t("dsc", T, U8)
+        lift_sb = t("lift_sb", LIFT_WINDOW)
+        w1_raw = t("w1_raw", PACK * R)
+        wo_raw = t("wo_raw", PACK * R)
+        dy_raw = t("dy_raw", PACK * M)
+        og_sb = t("og_sb", 1)
+        base_sb = t("base_sb", J)
+        s1 = t("s1", J)
+        xs1 = t("xs1", J)
+
+        nc.gpsimd.memset(tsc[:].bitcast(I32), 0)
+        nc.vector.memset(dsc[:].bitcast(I32), 0)
+        nc.vector.memset(lift_sb[:, U:], 0.0)
+        nc.gpsimd.memset(s1[:], 0.0)
+        nc.gpsimd.memset(xs1[:], 0.0)
+
+        def load_scales(tile, scales):
+            for q in range(4):
+                nc.sync.dma_start(out=tile[32 * q:32 * q + 4, :].bitcast(I32), in_=scales[0, 4 * q:4 * q + 4, :].bitcast(I32))
+
+        def load_rows(tile, rows):
+            nc.sync.dma_start(out=tile[:], in_=rows.rearrange("(p j) w -> p (j w)", j=PACK))
+
+        nc.sync.dma_start(slots[:], offs)
+        nc.sync.dma_start(out=tw[:].bitcast(I32), in_=tab_words[0].bitcast(I32))
+        load_scales(tsc, tab_scales)
+        load_rows(w1_raw, w1)
+        nc.sync.dma_start(lifts[:], offs2)
+        nc.sync.dma_start(out=lift_sb[:, :U], in_=lift)
+        load_scales(dsc, dtab_scales)
+        nc.sync.dma_start(out=dw[:].bitcast(I32), in_=dtab_words[0].bitcast(I32))
+        load_rows(dy_raw, dy)
+        load_rows(wo_raw, wo)
+        nc.sync.dma_start(picks[:], offs3)
+        nc.sync.dma_start(out=og_sb[:], in_=og)
+        nc.sync.dma_start(out=base_sb[:], in_=base)
+
+        def interleave(name, raw, width):
+            grouped = t(name, PACK * width, BF16)
+            nc.scalar.copy(out=grouped[:].rearrange("p (w j) -> p w j", j=PACK),
+                           in_=raw[:].rearrange("p (j w) -> p w j", j=PACK))
+            return grouped
+
+        def quantise(name, grouped, width):
+            codes = t(name + "_codes", width, U32)
+            plane = t(name + "_plane", width, U8)
+            nc.vector.quantize_mx(out=codes[:].bitcast(FP8X4), scales=plane[:], in_=grouped[:])
+            return codes, plane
+
+        w1_g = interleave("w1_g", w1_raw, R)
+        e = t("e", J)
+        nc.scalar.activation(e[:], lift_sb[:].indirect(lifts[:]), ACT.Exp)
+
+        gw = t("gw", J, U16)
+        gsc = t("gsc", J, U8)
+        nc.vector.tensor_copy(gw[:], tw[:].indirect(slots[:]))
+        nc.vector.tensor_copy(gsc[:], tsc[:].indirect(slots[:]))
+        w1_c, w1_s = quantise("w1", w1_g, R)
+        a_ps = ps.tile([P, J], F32, name="a_ps")
+        nc.tensor.matmul_mx(out=a_ps[:], lhsT=w1_c[:].bitcast(FP8X4), lhsT_scale=w1_s[:],
+                            rhs=gw[:].bitcast(FP4X4), rhs_scale=gsc[:], start=True, stop=True)
+        h1 = t("h1", J)
+        nc.scalar.activation(h1[:], a_ps[:], ACT.Tanh)
+        sq = t("sq", J)
+        nc.scalar.activation(sq[:], h1[:], ACT.Square)
+
+        gdw = t("gdw", J, U16)
+        gdsc = t("gdsc", J, U8)
+        nc.vector.tensor_copy(gdsc[:], dsc[:].indirect(slots[:]))
+        nc.vector.tensor_copy(gdw[:], dw[:].indirect(slots[:]))
+        ta_ps = ps.tile([P, J], F32, name="ta_ps")
+        nc.tensor.matmul_mx(out=ta_ps[:], lhsT=w1_c[:].bitcast(FP8X4), lhsT_scale=w1_s[:],
+                            rhs=gdw[:].bitcast(FP4X4), rhs_scale=gdsc[:], start=True, stop=True)
+
+        dy_g = interleave("dy_g", dy_raw, M)
+        wo_g = interleave("wo_g", wo_raw, R)
+
+        h2 = t("h2", J)
+        nc.vector.tensor_tensor(h2[:], h1[:], e[:], MULT)
+        ned = t("ned", J)
+        nc.vector.scalar_tensor_tensor(ned[:], sq[:], 1.0, e[:], SUB, MULT)
+        g = t("g", M)
+        nc.vector.tensor_copy(g[:], h2[:].indirect(picks[:]))
+        th = t("th", M)
+        nc.scalar.activation(th[:], g[:], ACT.Tanh, scale=0.5)
+        q = t("q", M)
+        nc.scalar.activation(q[:], th[:], ACT.Square, scale=0.5)
+        sg = t("sg", M)
+        nc.scalar.activation(sg[:], th[:], ACT.Copy, bias=0.5, scale=0.5)
+
+        dy_c, dy_s = quantise("dy", dy_g, M)
+        wo_c, wo_s = quantise("wo", wo_g, R)
+        c_ps = ps.tile([P, M], F32, name="c_ps")
+        nc.tensor.matmul_mx(out=c_ps[:], lhsT=wo_c[:].bitcast(FP8X4), lhsT_scale=wo_s[:],
+                            rhs=dy_c[:].bitcast(FP8X4), rhs_scale=dy_s[:], start=True, stop=True)
+        c0 = t("c0", M)
+        nc.scalar.copy(c0[:], c_ps[:])
+        nw = t("nw", M)
+        nc.scalar.activation(nw[:], q[:], ACT.Copy, bias=-0.25, scale=1.0)
+
+        xh2 = t("xh2", J, tag="dy_g")
+        nc.vector.scalar_tensor_tensor(xh2[:], ta_ps[:], -1.0, ned[:], MULT, MULT)
+        npw = t("npw", M, tag="wo_g")
+        nc.vector.scalar_tensor_tensor(npw[:], q[:], 0.25, g[:], SUB, MULT)
+        m = t("m", M)
+        nc.vector.tensor_tensor(m[:], g[:], th[:], MULT)
+        f1 = t("f1", M)
+        nc.vector.tensor_tensor(f1[:], sg[:], npw[:], SUB)
+        xc = t("xc", M)
+        nc.vector.tensor_tensor(xc[:], xh2[:].indirect(picks[:]), c0[:], MULT)
+        y = t("y", M)
+        nc.vector.scalar_tensor_tensor(y[:], m[:], 2.0, xc[:], SUB, MULT)
+        nc.vector.tensor_tensor(s1[:].indirect(picks[:]), f1[:], xc[:], MULT)
+        nc.vector.tensor_tensor(xs1[:].indirect(picks[:]), y[:], nw[:], MULT)
+
+        nog = t("nog", 1)
+        nc.gpsimd.tensor_scalar(nog[:], og_sb[:], -1.0, 0.0, MULT, ADD)
+        nog2 = t("nog2", 1)
+        nc.gpsimd.tensor_scalar(nog2[:], og_sb[:], -2.0, 0.0, MULT, ADD)
+        t2 = t("t2", J)
+        t1 = t("t1", J)
+        u = t("u", J)
+        res = t("res", J)
+        nc.vector.scalar_tensor_tensor(t2[:], s1[:], nog2[:], h1[:], MULT, MULT)
+        nc.vector.scalar_tensor_tensor(t1[:], xs1[:], nog[:], ned[:], MULT, MULT)
+        half = J // 2
+        for c in range(2):
+            cols = slice(c * half, (c + 1) * half)
+            nc.vector.tensor_tensor(u[:, cols], t2[:, cols], base_sb[:, cols], ADD)
+        for c in range(2):
+            cols = slice(c * half, (c + 1) * half)
+            nc.vector.tensor_tensor(res[:, cols], t1[:, cols], u[:, cols], ADD)
+            nc.sync.dma_start(out=out[:, cols], in_=res[:, cols])

@@ -1,6 +1,7 @@
 from contextlib import ExitStack
 
 import concourse.mybir as mybir
+from concourse.masks import make_identity
 
 K, R, F, T, J, U, M = 512, 128, 512, 2048, 512, 1024, 256
 FLOPS = 2 * R * (2 * K * J + F * M)
@@ -28,6 +29,7 @@ def tile_attend_hvliftedpicks_kernel(tc, tab_words, tab_scales, w1, lift, wo, dy
     nc = tc.nc
     with ExitStack() as ctx:
         sb = ctx.enter_context(tc.tile_pool(name="sb", bufs=1))
+        shared = ctx.enter_context(tc.tile_pool(name="shared", bufs=1))
         ps = ctx.enter_context(tc.psum_pool(name="ps", bufs=1))
 
         def t(name, cols, dtype=F32, tag=None):
@@ -38,7 +40,7 @@ def tile_attend_hvliftedpicks_kernel(tc, tab_words, tab_scales, w1, lift, wo, dy
         picks = t("picks", M // 16, U16)
         tw = t("tw", T, U16)
         tsc = t("tsc", T, U8)
-        dw = t("dw", T, U16)
+        dw = shared.tile([P, T], U16, name="dw", offset=0)
         dsc = t("dsc", T, U8)
         lift_sb = t("lift_sb", LIFT_WINDOW)
         w1_raw = t("w1_raw", PACK * R)
@@ -55,20 +57,20 @@ def tile_attend_hvliftedpicks_kernel(tc, tab_words, tab_scales, w1, lift, wo, dy
         nc.gpsimd.memset(s1[:], 0.0)
         nc.gpsimd.memset(xs1[:], 0.0)
 
-        def load_scales(tile, scales):
+        def load_scales(queue, tile, scales):
             for q in range(4):
-                nc.sync.dma_start(out=tile[32 * q:32 * q + 4, :].bitcast(I32), in_=scales[0, 4 * q:4 * q + 4, :].bitcast(I32))
+                queue.dma_start(out=tile[32 * q:32 * q + 4, :].bitcast(I32), in_=scales[0, 4 * q:4 * q + 4, :].bitcast(I32))
 
         def load_rows(tile, rows):
             nc.sync.dma_start(out=tile[:], in_=rows.rearrange("(p j) w -> p (j w)", j=PACK))
 
         nc.sync.dma_start(slots[:], offs)
         nc.sync.dma_start(out=tw[:].bitcast(I32), in_=tab_words[0].bitcast(I32))
-        load_scales(tsc, tab_scales)
+        load_scales(nc.sync, tsc, tab_scales)
         load_rows(w1_raw, w1)
-        nc.sync.dma_start(lifts[:], offs2)
         nc.sync.dma_start(out=lift_sb[:, :U], in_=lift)
-        load_scales(dsc, dtab_scales)
+        nc.sync.dma_start(lifts[:], offs2)
+        load_scales(nc.sync, dsc, dtab_scales)
         nc.sync.dma_start(out=dw[:].bitcast(I32), in_=dtab_words[0].bitcast(I32))
         load_rows(dy_raw, dy)
         load_rows(wo_raw, wo)
@@ -78,8 +80,8 @@ def tile_attend_hvliftedpicks_kernel(tc, tab_words, tab_scales, w1, lift, wo, dy
 
         def interleave(name, raw, width):
             grouped = t(name, PACK * width, BF16)
-            nc.scalar.copy(out=grouped[:].rearrange("p (w j) -> p w j", j=PACK),
-                           in_=raw[:].rearrange("p (j w) -> p w j", j=PACK))
+            nc.scalar.copy(out=grouped[:].rearrange("p (c i j) -> p c j i", i=4, j=PACK),
+                           in_=raw[:].rearrange("p (j c i) -> p c j i", i=4, j=PACK))
             return grouped
 
         def quantise(name, grouped, width):
@@ -100,7 +102,7 @@ def tile_attend_hvliftedpicks_kernel(tc, tab_words, tab_scales, w1, lift, wo, dy
         a_ps = ps.tile([P, J], F32, name="a_ps")
         nc.tensor.matmul_mx(out=a_ps[:], lhsT=w1_c[:].bitcast(FP8X4), lhsT_scale=w1_s[:],
                             rhs=gw[:].bitcast(FP4X4), rhs_scale=gsc[:], start=True, stop=True)
-        h1 = t("h1", J)
+        h1 = t("h1", J, tag="lift_sb")
         nc.scalar.activation(h1[:], a_ps[:], ACT.Tanh)
         sq = t("sq", J)
         nc.scalar.activation(sq[:], h1[:], ACT.Square)
@@ -116,59 +118,73 @@ def tile_attend_hvliftedpicks_kernel(tc, tab_words, tab_scales, w1, lift, wo, dy
         dy_g = interleave("dy_g", dy_raw, M)
         wo_g = interleave("wo_g", wo_raw, R)
 
-        h2 = t("h2", J)
+        h2 = shared.tile([P, J], F32, name="h2", offset=0)
         nc.vector.tensor_tensor(h2[:], h1[:], e[:], MULT)
-        ned = t("ned", J)
+        ned = shared.tile([P, J], F32, name="ned", offset=4 * J)
         nc.vector.scalar_tensor_tensor(ned[:], sq[:], 1.0, e[:], SUB, MULT)
         g = t("g", M)
         nc.vector.tensor_copy(g[:], h2[:].indirect(picks[:]))
-        th = t("th", M)
+        th = t("th", M, tag="wo_raw")
         nc.scalar.activation(th[:], g[:], ACT.Tanh, scale=0.5)
         q = t("q", M)
         nc.scalar.activation(q[:], th[:], ACT.Square, scale=0.5)
         sg = t("sg", M)
         nc.scalar.activation(sg[:], th[:], ACT.Copy, bias=0.5, scale=0.5)
 
+        w2 = t("w2", M)
+        nc.scalar.activation(w2[:], q[:], ACT.Copy, bias=0.5, scale=-2.0)
+
         dy_c, dy_s = quantise("dy", dy_g, M)
         wo_c, wo_s = quantise("wo", wo_g, R)
         c_ps = ps.tile([P, M], F32, name="c_ps")
         nc.tensor.matmul_mx(out=c_ps[:], lhsT=wo_c[:].bitcast(FP8X4), lhsT_scale=wo_s[:],
                             rhs=dy_c[:].bitcast(FP8X4), rhs_scale=dy_s[:], start=True, stop=True)
+
         c0 = t("c0", M)
         nc.scalar.copy(c0[:], c_ps[:])
-        nw = t("nw", M)
-        nc.scalar.activation(nw[:], q[:], ACT.Copy, bias=-0.25, scale=1.0)
-
         xh2 = t("xh2", J, tag="dy_g")
         nc.vector.scalar_tensor_tensor(xh2[:], ta_ps[:], -1.0, ned[:], MULT, MULT)
         npw = t("npw", M, tag="wo_g")
         nc.vector.scalar_tensor_tensor(npw[:], q[:], 0.25, g[:], SUB, MULT)
-        m = t("m", M)
-        nc.vector.tensor_tensor(m[:], g[:], th[:], MULT)
-        f1 = t("f1", M)
-        nc.vector.tensor_tensor(f1[:], sg[:], npw[:], SUB)
         xc = t("xc", M)
         nc.vector.tensor_tensor(xc[:], xh2[:].indirect(picks[:]), c0[:], MULT)
-        y = t("y", M)
-        nc.vector.scalar_tensor_tensor(y[:], m[:], 2.0, xc[:], SUB, MULT)
+        f1 = t("f1", M)
+        nc.vector.tensor_tensor(f1[:], sg[:], npw[:], SUB)
+        m = t("m", M)
+        nc.vector.tensor_tensor(m[:], npw[:], th[:], MULT)
         nc.vector.tensor_tensor(s1[:].indirect(picks[:]), f1[:], xc[:], MULT)
-        nc.vector.tensor_tensor(xs1[:].indirect(picks[:]), y[:], nw[:], MULT)
+        f2 = t("f2", M, tag="f1")
+        nc.vector.tensor_tensor(f2[:], m[:], w2[:], ADD)
 
         nog = t("nog", 1)
         nc.gpsimd.tensor_scalar(nog[:], og_sb[:], -1.0, 0.0, MULT, ADD)
         nog2 = t("nog2", 1)
         nc.gpsimd.tensor_scalar(nog2[:], og_sb[:], -2.0, 0.0, MULT, ADD)
+        ident = t("ident", P)
+        make_identity(nc, ident[:])
         t2 = t("t2", J)
         t1 = t("t1", J)
-        u = t("u", J)
         res = t("res", J)
         nc.vector.scalar_tensor_tensor(t2[:], s1[:], nog2[:], h1[:], MULT, MULT)
-        nc.vector.scalar_tensor_tensor(t1[:], xs1[:], nog[:], ned[:], MULT, MULT)
+        nc.vector.tensor_tensor(xs1[:].indirect(picks[:]), f2[:], xc[:], MULT)
+
+        turned = t("turned", J)
         half = J // 2
+        u_ps = [ps.tile([P, half], F32, name="u_ps", tag=tag) for tag in ("a_ps", "c_ps")]
+        blocks = [slice(c * P, (c + 1) * P) for c in range(J // P)]
+        sums = [ps.tile([P, P], F32, name="sum%d" % c) for c in range(J // P)]
+        for c, cols in enumerate(blocks):
+            nc.tensor.matmul(sums[c][:], base_sb[:, cols], ident[:], start=True, stop=False, is_transpose=True)
+        for c, cols in enumerate(blocks):
+            nc.tensor.matmul(sums[c][:], t2[:, cols], ident[:], start=False, stop=True, is_transpose=True)
+            nc.scalar.copy(turned[:, cols], sums[c][:])
+        for c, cols in enumerate(blocks):
+            nc.tensor.transpose(u_ps[c // 2][:, blocks[c % 2]], turned[:, cols], ident[:])
+
         for c in range(2):
             cols = slice(c * half, (c + 1) * half)
-            nc.vector.tensor_tensor(u[:, cols], t2[:, cols], base_sb[:, cols], ADD)
+            nc.vector.scalar_tensor_tensor(t1[:, cols], xs1[:, cols], nog[:], ned[:, cols], MULT, MULT)
         for c in range(2):
             cols = slice(c * half, (c + 1) * half)
-            nc.vector.tensor_tensor(res[:, cols], t1[:, cols], u[:, cols], ADD)
+            nc.vector.tensor_tensor(res[:, cols], t1[:, cols], u_ps[c][:], ADD)
             nc.sync.dma_start(out=out[:, cols], in_=res[:, cols])

@@ -51,11 +51,11 @@ def tile_attend_hvliftedpicks_kernel(tc, tab_words, tab_scales, w1, lift, wo, dy
         s1 = t("s1", J)
         xs1 = t("xs1", J)
 
-        nc.gpsimd.memset(tsc[:].bitcast(I32), 0)
+        nc.vector.memset(tsc[:].bitcast(I32), 0)
         nc.vector.memset(dsc[:].bitcast(I32), 0)
         nc.vector.memset(lift_sb[:, U:], 0.0)
-        nc.gpsimd.memset(s1[:], 0.0)
-        nc.gpsimd.memset(xs1[:], 0.0)
+        nc.vector.memset(s1[:], 0.0)
+        nc.vector.memset(xs1[:], 0.0)
 
         def load_scales(queue, tile, scales):
             for q in range(4):
@@ -129,10 +129,10 @@ def tile_attend_hvliftedpicks_kernel(tc, tab_words, tab_scales, w1, lift, wo, dy
         q = t("q", M)
         nc.scalar.activation(q[:], th[:], ACT.Square, scale=0.5)
         sg = t("sg", M)
-        nc.scalar.activation(sg[:], th[:], ACT.Copy, bias=0.5, scale=0.5)
+        nc.scalar.activation(sg[:], th[:], ACT.Copy, bias=-1.0, scale=-1.0)
 
         w2 = t("w2", M)
-        nc.scalar.activation(w2[:], q[:], ACT.Copy, bias=0.5, scale=-2.0)
+        nc.scalar.activation(w2[:], q[:], ACT.Copy, bias=-0.5, scale=2.0)
 
         dy_c, dy_s = quantise("dy", dy_g, M)
         wo_c, wo_s = quantise("wo", wo_g, R)
@@ -149,23 +149,19 @@ def tile_attend_hvliftedpicks_kernel(tc, tab_words, tab_scales, w1, lift, wo, dy
         xc = t("xc", M)
         nc.vector.tensor_tensor(xc[:], xh2[:].indirect(picks[:]), c0[:], MULT)
         f1 = t("f1", M)
-        nc.vector.tensor_tensor(f1[:], sg[:], npw[:], SUB)
+        nc.vector.scalar_tensor_tensor(f1[:], npw[:], 2.0, sg[:], MULT, ADD)
         m = t("m", M)
         nc.vector.tensor_tensor(m[:], npw[:], th[:], MULT)
         nc.vector.tensor_tensor(s1[:].indirect(picks[:]), f1[:], xc[:], MULT)
         f2 = t("f2", M, tag="f1")
-        nc.vector.tensor_tensor(f2[:], m[:], w2[:], ADD)
+        nc.vector.tensor_tensor(f2[:], w2[:], m[:], SUB)
 
-        nog = t("nog", 1)
-        nc.gpsimd.tensor_scalar(nog[:], og_sb[:], -1.0, 0.0, MULT, ADD)
-        nog2 = t("nog2", 1)
-        nc.gpsimd.tensor_scalar(nog2[:], og_sb[:], -2.0, 0.0, MULT, ADD)
         ident = t("ident", P)
         make_identity(nc, ident[:])
         t2 = t("t2", J)
         t1 = t("t1", J)
         res = t("res", J)
-        nc.vector.scalar_tensor_tensor(t2[:], s1[:], nog2[:], h1[:], MULT, MULT)
+        nc.vector.scalar_tensor_tensor(t2[:], s1[:], og_sb[:], h1[:], MULT, MULT)
         nc.vector.tensor_tensor(xs1[:].indirect(picks[:]), f2[:], xc[:], MULT)
 
         turned = t("turned", J)
@@ -183,8 +179,8 @@ def tile_attend_hvliftedpicks_kernel(tc, tab_words, tab_scales, w1, lift, wo, dy
 
         for c in range(2):
             cols = slice(c * half, (c + 1) * half)
-            nc.vector.scalar_tensor_tensor(t1[:, cols], xs1[:, cols], nog[:], ned[:, cols], MULT, MULT)
+            nc.vector.scalar_tensor_tensor(t1[:, cols], xs1[:, cols], og_sb[:], ned[:, cols], MULT, MULT)
         for c in range(2):
             cols = slice(c * half, (c + 1) * half)
             nc.vector.tensor_tensor(res[:, cols], t1[:, cols], u_ps[c][:], ADD)
-            nc.sync.dma_start(out=out[:, cols], in_=res[:, cols])
+            (nc.sync, nc.scalar)[c].dma_start(out=out[:, cols], in_=res[:, cols])

@@ -21,7 +21,12 @@ SUB = mybir.AluOpType.subtract
 
 P = 128
 PACK = 4
-LIFT_WINDOW = 2048
+GROUP = 16
+QUADRANT = 32
+SCALE_ROWS = 4
+RUN = 4
+LIFT_WINDOW = 2 * U
+HALF = J // 2
 
 
 def tile_attend_hvliftedpicks_kernel(tc, tab_words, tab_scales, w1, lift, wo, dy, dtab_words, dtab_scales, og, base,
@@ -32,46 +37,48 @@ def tile_attend_hvliftedpicks_kernel(tc, tab_words, tab_scales, w1, lift, wo, dy
         shared = ctx.enter_context(tc.tile_pool(name="shared", bufs=1))
         ps = ctx.enter_context(tc.psum_pool(name="ps", bufs=1))
 
-        def t(name, cols, dtype=F32, tag=None):
-            return sb.tile([P, cols], dtype, name=name, tag=tag or name, align_bytes=64)
+        def sbuf(name, cols, dtype=F32, on=None):
+            return sb.tile([P, cols], dtype, name=name, tag=on or name, align_bytes=64)
 
-        slots = t("slots", J // 16, U16)
-        lifts = t("lifts", J // 16, U16)
-        picks = t("picks", M // 16, U16)
-        tw = t("tw", T, U16)
-        tsc = t("tsc", T, U8)
-        dw = shared.tile([P, T], U16, name="dw", offset=0)
-        dsc = t("dsc", T, U8)
-        lift_sb = t("lift_sb", LIFT_WINDOW)
-        w1_raw = t("w1_raw", PACK * R)
-        wo_raw = t("wo_raw", PACK * R)
-        dy_raw = t("dy_raw", PACK * M)
-        og_sb = t("og_sb", 1)
-        base_sb = t("base_sb", J)
-        s1 = t("s1", J)
-        xs1 = t("xs1", J)
+        slots = sbuf("slots", J // GROUP, U16)
+        lifts = sbuf("lifts", J // GROUP, U16)
+        picks = sbuf("picks", M // GROUP, U16)
+        tab_w = sbuf("tab_w", T, U16)
+        tab_s = sbuf("tab_s", T, U8)
+        dtab_w = shared.tile([P, T], U16, name="dtab_w", offset=0)
+        dtab_s = sbuf("dtab_s", T, U8)
+        lift_sb = sbuf("lift_sb", LIFT_WINDOW)
+        w1_raw = sbuf("w1_raw", PACK * R)
+        wo_raw = sbuf("wo_raw", PACK * R)
+        dy_raw = sbuf("dy_raw", PACK * M)
+        og_sb = sbuf("og_sb", 1)
+        base_sb = sbuf("base_sb", J)
+        placed_e1 = sbuf("placed_e1", J)
+        placed_xe1 = sbuf("placed_xe1", J)
 
-        nc.vector.memset(tsc[:].bitcast(I32), 0)
-        nc.vector.memset(dsc[:].bitcast(I32), 0)
+        nc.vector.memset(tab_s[:].bitcast(I32), 0)
+        nc.vector.memset(dtab_s[:].bitcast(I32), 0)
         nc.vector.memset(lift_sb[:, U:], 0.0)
-        nc.vector.memset(s1[:], 0.0)
-        nc.vector.memset(xs1[:], 0.0)
+        nc.vector.memset(placed_e1[:], 0.0)
+        nc.vector.memset(placed_xe1[:], 0.0)
 
-        def load_scales(queue, tile, scales):
-            for q in range(4):
-                queue.dma_start(out=tile[32 * q:32 * q + 4, :].bitcast(I32), in_=scales[0, 4 * q:4 * q + 4, :].bitcast(I32))
+        def load_scales(tile, scales):
+            for quad in range(P // QUADRANT):
+                rows = scales[0, SCALE_ROWS * quad:SCALE_ROWS * (quad + 1), :]
+                nc.sync.dma_start(out=tile[QUADRANT * quad:QUADRANT * quad + SCALE_ROWS, :].bitcast(I32),
+                                  in_=rows.bitcast(I32))
 
         def load_rows(tile, rows):
             nc.sync.dma_start(out=tile[:], in_=rows.rearrange("(p j) w -> p (j w)", j=PACK))
 
         nc.sync.dma_start(slots[:], offs)
-        nc.sync.dma_start(out=tw[:].bitcast(I32), in_=tab_words[0].bitcast(I32))
-        load_scales(nc.sync, tsc, tab_scales)
+        nc.sync.dma_start(out=tab_w[:].bitcast(I32), in_=tab_words[0].bitcast(I32))
+        load_scales(tab_s, tab_scales)
         load_rows(w1_raw, w1)
         nc.sync.dma_start(out=lift_sb[:, :U], in_=lift)
         nc.sync.dma_start(lifts[:], offs2)
-        load_scales(nc.sync, dsc, dtab_scales)
-        nc.sync.dma_start(out=dw[:].bitcast(I32), in_=dtab_words[0].bitcast(I32))
+        load_scales(dtab_s, dtab_scales)
+        nc.sync.dma_start(out=dtab_w[:].bitcast(I32), in_=dtab_words[0].bitcast(I32))
         load_rows(dy_raw, dy)
         load_rows(wo_raw, wo)
         nc.sync.dma_start(picks[:], offs3)
@@ -79,108 +86,107 @@ def tile_attend_hvliftedpicks_kernel(tc, tab_words, tab_scales, w1, lift, wo, dy
         nc.sync.dma_start(out=base_sb[:], in_=base)
 
         def interleave(name, raw, width):
-            grouped = t(name, PACK * width, BF16)
-            nc.scalar.copy(out=grouped[:].rearrange("p (c i j) -> p c j i", i=4, j=PACK),
-                           in_=raw[:].rearrange("p (j c i) -> p c j i", i=4, j=PACK))
+            grouped = sbuf(name, PACK * width, BF16)
+            nc.scalar.copy(out=grouped[:].rearrange("p (c i j) -> p c j i", i=RUN, j=PACK),
+                           in_=raw[:].rearrange("p (j c i) -> p c j i", i=RUN, j=PACK))
             return grouped
 
         def quantise(name, grouped, width):
-            codes = t(name + "_codes", width, U32)
-            plane = t(name + "_plane", width, U8)
-            nc.vector.quantize_mx(out=codes[:].bitcast(FP8X4), scales=plane[:], in_=grouped[:])
-            return codes, plane
+            words = sbuf(name + "_words", width, U32)
+            scales = sbuf(name + "_scales", width, U8)
+            nc.vector.quantize_mx(out=words[:].bitcast(FP8X4), scales=scales[:], in_=grouped[:])
+            return words, scales
 
-        w1_g = interleave("w1_g", w1_raw, R)
-        e = t("e", J)
-        nc.scalar.activation(e[:], lift_sb[:].indirect(lifts[:]), ACT.Exp)
+        w1_bf = interleave("w1_bf", w1_raw, R)
+        lifted = sbuf("lifted", J)
+        nc.scalar.activation(lifted[:], lift_sb[:].indirect(lifts[:]), ACT.Exp)
 
-        gw = t("gw", J, U16)
-        gsc = t("gsc", J, U8)
-        nc.vector.tensor_copy(gw[:], tw[:].indirect(slots[:]))
-        nc.vector.tensor_copy(gsc[:], tsc[:].indirect(slots[:]))
-        w1_c, w1_s = quantise("w1", w1_g, R)
+        tab_gw = sbuf("tab_gw", J, U16)
+        tab_gs = sbuf("tab_gs", J, U8)
+        nc.vector.tensor_copy(tab_gw[:], tab_w[:].indirect(slots[:]))
+        nc.vector.tensor_copy(tab_gs[:], tab_s[:].indirect(slots[:]))
+        w1_words, w1_scales = quantise("w1", w1_bf, R)
         a_ps = ps.tile([P, J], F32, name="a_ps")
-        nc.tensor.matmul_mx(out=a_ps[:], lhsT=w1_c[:].bitcast(FP8X4), lhsT_scale=w1_s[:],
-                            rhs=gw[:].bitcast(FP4X4), rhs_scale=gsc[:], start=True, stop=True)
-        h1 = t("h1", J, tag="lift_sb")
+        nc.tensor.matmul_mx(out=a_ps[:], lhsT=w1_words[:].bitcast(FP8X4), lhsT_scale=w1_scales[:],
+                            rhs=tab_gw[:].bitcast(FP4X4), rhs_scale=tab_gs[:], start=True, stop=True)
+        h1 = sbuf("h1", J, on="lift_sb")
         nc.scalar.activation(h1[:], a_ps[:], ACT.Tanh)
-        sq = t("sq", J)
-        nc.scalar.activation(sq[:], h1[:], ACT.Square)
+        h1_sq = sbuf("h1_sq", J)
+        nc.scalar.activation(h1_sq[:], h1[:], ACT.Square)
 
-        gdw = t("gdw", J, U16)
-        gdsc = t("gdsc", J, U8)
-        nc.vector.tensor_copy(gdsc[:], dsc[:].indirect(slots[:]))
-        nc.vector.tensor_copy(gdw[:], dw[:].indirect(slots[:]))
+        dtab_gw = sbuf("dtab_gw", J, U16)
+        dtab_gs = sbuf("dtab_gs", J, U8)
+        nc.vector.tensor_copy(dtab_gs[:], dtab_s[:].indirect(slots[:]))
+        nc.vector.tensor_copy(dtab_gw[:], dtab_w[:].indirect(slots[:]))
         ta_ps = ps.tile([P, J], F32, name="ta_ps")
-        nc.tensor.matmul_mx(out=ta_ps[:], lhsT=w1_c[:].bitcast(FP8X4), lhsT_scale=w1_s[:],
-                            rhs=gdw[:].bitcast(FP4X4), rhs_scale=gdsc[:], start=True, stop=True)
+        nc.tensor.matmul_mx(out=ta_ps[:], lhsT=w1_words[:].bitcast(FP8X4), lhsT_scale=w1_scales[:],
+                            rhs=dtab_gw[:].bitcast(FP4X4), rhs_scale=dtab_gs[:], start=True, stop=True)
 
-        dy_g = interleave("dy_g", dy_raw, M)
-        wo_g = interleave("wo_g", wo_raw, R)
+        dy_bf = interleave("dy_bf", dy_raw, M)
+        wo_bf = interleave("wo_bf", wo_raw, R)
 
         h2 = shared.tile([P, J], F32, name="h2", offset=0)
-        nc.vector.tensor_tensor(h2[:], h1[:], e[:], MULT)
-        ned = shared.tile([P, J], F32, name="ned", offset=4 * J)
-        nc.vector.scalar_tensor_tensor(ned[:], sq[:], 1.0, e[:], SUB, MULT)
-        g = t("g", M)
+        nc.vector.tensor_tensor(h2[:], h1[:], lifted[:], MULT)
+        neg_ed = shared.tile([P, J], F32, name="neg_ed", offset=4 * J)
+        nc.vector.scalar_tensor_tensor(neg_ed[:], h1_sq[:], 1.0, lifted[:], SUB, MULT)
+        g = sbuf("g", M)
         nc.vector.tensor_copy(g[:], h2[:].indirect(picks[:]))
-        th = t("th", M, tag="wo_raw")
+
+        th = sbuf("th", M, on="wo_raw")
         nc.scalar.activation(th[:], g[:], ACT.Tanh, scale=0.5)
-        q = t("q", M)
-        nc.scalar.activation(q[:], th[:], ACT.Square, scale=0.5)
-        sg = t("sg", M)
-        nc.scalar.activation(sg[:], th[:], ACT.Copy, bias=-1.0, scale=-1.0)
+        th_sq = sbuf("th_sq", M)
+        nc.scalar.activation(th_sq[:], th[:], ACT.Square, scale=0.5)
 
-        w2 = t("w2", M)
-        nc.scalar.activation(w2[:], q[:], ACT.Copy, bias=-0.5, scale=2.0)
+        dy_words, dy_scales = quantise("dy", dy_bf, M)
+        wo_words, wo_scales = quantise("wo", wo_bf, R)
+        c0_ps = ps.tile([P, M], F32, name="c0_ps")
+        nc.tensor.matmul_mx(out=c0_ps[:], lhsT=wo_words[:].bitcast(FP8X4), lhsT_scale=wo_scales[:],
+                            rhs=dy_words[:].bitcast(FP8X4), rhs_scale=dy_scales[:], start=True, stop=True)
+        c0 = sbuf("c0", M)
+        nc.scalar.copy(c0[:], c0_ps[:])
+        neg_2s = sbuf("neg_2s", M)
+        nc.scalar.activation(neg_2s[:], th[:], ACT.Copy, bias=-1.0, scale=-1.0)
+        neg_2w = sbuf("neg_2w", M)
+        nc.scalar.activation(neg_2w[:], th_sq[:], ACT.Copy, bias=-0.5, scale=2.0)
 
-        dy_c, dy_s = quantise("dy", dy_g, M)
-        wo_c, wo_s = quantise("wo", wo_g, R)
-        c_ps = ps.tile([P, M], F32, name="c_ps")
-        nc.tensor.matmul_mx(out=c_ps[:], lhsT=wo_c[:].bitcast(FP8X4), lhsT_scale=wo_s[:],
-                            rhs=dy_c[:].bitcast(FP8X4), rhs_scale=dy_s[:], start=True, stop=True)
+        xh2 = sbuf("xh2", J, on="wo_bf")
+        nc.vector.scalar_tensor_tensor(xh2[:], ta_ps[:], -1.0, neg_ed[:], MULT, MULT)
+        neg_gw = sbuf("neg_gw", M, on="dy_bf")
+        nc.vector.scalar_tensor_tensor(neg_gw[:], th_sq[:], 0.25, g[:], SUB, MULT)
+        xc0 = sbuf("xc0", M)
+        nc.vector.tensor_tensor(xc0[:], xh2[:].indirect(picks[:]), c0[:], MULT)
+        neg_2f1 = sbuf("neg_2f1", M)
+        nc.vector.scalar_tensor_tensor(neg_2f1[:], neg_gw[:], 2.0, neg_2s[:], MULT, ADD)
+        neg_gwth = sbuf("neg_gwth", M)
+        nc.vector.tensor_tensor(neg_gwth[:], neg_gw[:], th[:], MULT)
+        nc.vector.tensor_tensor(placed_e1[:].indirect(picks[:]), neg_2f1[:], xc0[:], MULT)
+        neg_f2 = sbuf("neg_f2", M, on="neg_2f1")
+        nc.vector.tensor_tensor(neg_f2[:], neg_2w[:], neg_gwth[:], SUB)
 
-        c0 = t("c0", M)
-        nc.scalar.copy(c0[:], c_ps[:])
-        xh2 = t("xh2", J, tag="dy_g")
-        nc.vector.scalar_tensor_tensor(xh2[:], ta_ps[:], -1.0, ned[:], MULT, MULT)
-        npw = t("npw", M, tag="wo_g")
-        nc.vector.scalar_tensor_tensor(npw[:], q[:], 0.25, g[:], SUB, MULT)
-        xc = t("xc", M)
-        nc.vector.tensor_tensor(xc[:], xh2[:].indirect(picks[:]), c0[:], MULT)
-        f1 = t("f1", M)
-        nc.vector.scalar_tensor_tensor(f1[:], npw[:], 2.0, sg[:], MULT, ADD)
-        m = t("m", M)
-        nc.vector.tensor_tensor(m[:], npw[:], th[:], MULT)
-        nc.vector.tensor_tensor(s1[:].indirect(picks[:]), f1[:], xc[:], MULT)
-        f2 = t("f2", M, tag="f1")
-        nc.vector.tensor_tensor(f2[:], w2[:], m[:], SUB)
-
-        ident = t("ident", P)
+        ident = sbuf("ident", P)
         make_identity(nc, ident[:])
-        t2 = t("t2", J)
-        t1 = t("t1", J)
-        res = t("res", J)
-        nc.vector.scalar_tensor_tensor(t2[:], s1[:], og_sb[:], h1[:], MULT, MULT)
-        nc.vector.tensor_tensor(xs1[:].indirect(picks[:]), f2[:], xc[:], MULT)
+        term_e1 = sbuf("term_e1", J)
+        term_xe1 = sbuf("term_xe1", J)
+        result = sbuf("result", J)
+        nc.vector.scalar_tensor_tensor(term_e1[:], placed_e1[:], og_sb[:], h1[:], MULT, MULT)
+        nc.vector.tensor_tensor(placed_xe1[:].indirect(picks[:]), neg_f2[:], xc0[:], MULT)
 
-        turned = t("turned", J)
-        half = J // 2
-        u_ps = [ps.tile([P, half], F32, name="u_ps", tag=tag) for tag in ("a_ps", "c_ps")]
-        blocks = [slice(c * P, (c + 1) * P) for c in range(J // P)]
-        sums = [ps.tile([P, P], F32, name="sum%d" % c) for c in range(J // P)]
-        for c, cols in enumerate(blocks):
-            nc.tensor.matmul(sums[c][:], base_sb[:, cols], ident[:], start=True, stop=False, is_transpose=True)
-        for c, cols in enumerate(blocks):
-            nc.tensor.matmul(sums[c][:], t2[:, cols], ident[:], start=False, stop=True, is_transpose=True)
-            nc.scalar.copy(turned[:, cols], sums[c][:])
-        for c, cols in enumerate(blocks):
-            nc.tensor.transpose(u_ps[c // 2][:, blocks[c % 2]], turned[:, cols], ident[:])
+        turned = sbuf("turned", J)
+        partial = [ps.tile([P, HALF], F32, name="partial", tag=bank) for bank in ("a_ps", "c0_ps")]
+        blocks = [slice(b * P, (b + 1) * P) for b in range(J // P)]
+        sums = [ps.tile([P, P], F32, name="sum%d" % b) for b in range(J // P)]
+        for b, cols in enumerate(blocks):
+            nc.tensor.matmul(sums[b][:], base_sb[:, cols], ident[:], start=True, stop=False, is_transpose=True)
+        for b, cols in enumerate(blocks):
+            nc.tensor.matmul(sums[b][:], term_e1[:, cols], ident[:], start=False, stop=True, is_transpose=True)
+            nc.scalar.copy(turned[:, cols], sums[b][:])
+        blocks_per_half = HALF // P
+        for b, cols in enumerate(blocks):
+            nc.tensor.transpose(partial[b // blocks_per_half][:, blocks[b % blocks_per_half]], turned[:, cols], ident[:])
 
-        for c in range(2):
-            cols = slice(c * half, (c + 1) * half)
-            nc.vector.scalar_tensor_tensor(t1[:, cols], xs1[:, cols], og_sb[:], ned[:, cols], MULT, MULT)
-        for c in range(2):
-            cols = slice(c * half, (c + 1) * half)
-            nc.vector.tensor_tensor(res[:, cols], t1[:, cols], u_ps[c][:], ADD)
-            (nc.sync, nc.scalar)[c].dma_start(out=out[:, cols], in_=res[:, cols])
+        halves = [slice(h * HALF, (h + 1) * HALF) for h in range(J // HALF)]
+        for cols in halves:
+            nc.vector.scalar_tensor_tensor(term_xe1[:, cols], placed_xe1[:, cols], og_sb[:], neg_ed[:, cols], MULT, MULT)
+        for cols, sum_ps, queue in zip(halves, partial, (nc.sync, nc.scalar)):
+            nc.vector.tensor_tensor(result[:, cols], term_xe1[:, cols], sum_ps[:], ADD)
+            queue.dma_start(out=out[:, cols], in_=result[:, cols])

from contextlib import ExitStack

import concourse.mybir as mybir
from concourse.masks import make_identity

K, R, F, T, J, U, M = 512, 128, 512, 2048, 512, 1024, 256
FLOPS = 2 * R * (2 * K * J + F * M)

F32 = mybir.dt.float32
BF16 = mybir.dt.bfloat16
I32 = mybir.dt.int32
U32 = mybir.dt.uint32
U16 = mybir.dt.uint16
U8 = mybir.dt.uint8
FP8X4 = mybir.dt.float8_e4m3fn_x4
FP4X4 = mybir.dt.float4_e2m1fn_x4
ACT = mybir.ActivationFunctionType
MULT = mybir.AluOpType.mult
ADD = mybir.AluOpType.add
SUB = mybir.AluOpType.subtract

P = 128
PACK = 4
GROUP = 16
QUADRANT = 32
SCALE_ROWS = 4
RUN = 4
LIFT_WINDOW = 2 * U
HALF = J // 2


def tile_attend_hvliftedpicks_kernel(tc, tab_words, tab_scales, w1, lift, wo, dy, dtab_words, dtab_scales, og, base,
                                      offs, offs2, offs3, out):
    nc = tc.nc
    with ExitStack() as ctx:
        sb = ctx.enter_context(tc.tile_pool(name="sb", bufs=1))
        shared = ctx.enter_context(tc.tile_pool(name="shared", bufs=1))
        ps = ctx.enter_context(tc.psum_pool(name="ps", bufs=1))

        def sbuf(name, cols, dtype=F32, on=None):
            return sb.tile([P, cols], dtype, name=name, tag=on or name, align_bytes=64)

        slots = sbuf("slots", J // GROUP, U16)
        lifts = sbuf("lifts", J // GROUP, U16)
        picks = sbuf("picks", M // GROUP, U16)
        tab_w = sbuf("tab_w", T, U16)
        tab_s = sbuf("tab_s", T, U8)
        dtab_w = shared.tile([P, T], U16, name="dtab_w", offset=0)
        dtab_s = sbuf("dtab_s", T, U8)
        lift_sb = sbuf("lift_sb", LIFT_WINDOW)
        w1_raw = sbuf("w1_raw", PACK * R)
        wo_raw = sbuf("wo_raw", PACK * R)
        dy_raw = sbuf("dy_raw", PACK * M)
        og_sb = sbuf("og_sb", 1)
        base_sb = sbuf("base_sb", J)
        placed_e1 = sbuf("placed_e1", J)
        placed_xe1 = sbuf("placed_xe1", J)

        nc.vector.memset(tab_s[:].bitcast(I32), 0)
        nc.vector.memset(dtab_s[:].bitcast(I32), 0)
        nc.vector.memset(lift_sb[:, U:], 0.0)
        nc.vector.memset(placed_e1[:], 0.0)
        nc.vector.memset(placed_xe1[:], 0.0)

        def load_scales(tile, scales):
            for quad in range(P // QUADRANT):
                rows = scales[0, SCALE_ROWS * quad:SCALE_ROWS * (quad + 1), :]
                nc.sync.dma_start(out=tile[QUADRANT * quad:QUADRANT * quad + SCALE_ROWS, :].bitcast(I32),
                                  in_=rows.bitcast(I32))

        def load_rows(tile, rows):
            nc.sync.dma_start(out=tile[:], in_=rows.rearrange("(p j) w -> p (j w)", j=PACK))

        nc.sync.dma_start(slots[:], offs)
        nc.sync.dma_start(out=tab_w[:].bitcast(I32), in_=tab_words[0].bitcast(I32))
        load_scales(tab_s, tab_scales)
        load_rows(w1_raw, w1)
        nc.sync.dma_start(out=lift_sb[:, :U], in_=lift)
        nc.sync.dma_start(lifts[:], offs2)
        load_scales(dtab_s, dtab_scales)
        nc.sync.dma_start(out=dtab_w[:].bitcast(I32), in_=dtab_words[0].bitcast(I32))
        load_rows(dy_raw, dy)
        load_rows(wo_raw, wo)
        nc.sync.dma_start(picks[:], offs3)
        nc.sync.dma_start(out=og_sb[:], in_=og)
        nc.sync.dma_start(out=base_sb[:], in_=base)

        def interleave(name, raw, width):
            grouped = sbuf(name, PACK * width, BF16)
            nc.scalar.copy(out=grouped[:].rearrange("p (c i j) -> p c j i", i=RUN, j=PACK),
                           in_=raw[:].rearrange("p (j c i) -> p c j i", i=RUN, j=PACK))
            return grouped

        def quantise(name, grouped, width):
            words = sbuf(name + "_words", width, U32)
            scales = sbuf(name + "_scales", width, U8)
            nc.vector.quantize_mx(out=words[:].bitcast(FP8X4), scales=scales[:], in_=grouped[:])
            return words, scales

        w1_bf = interleave("w1_bf", w1_raw, R)
        lifted = sbuf("lifted", J)
        nc.scalar.activation(lifted[:], lift_sb[:].indirect(lifts[:]), ACT.Exp)

        tab_gw = sbuf("tab_gw", J, U16)
        tab_gs = sbuf("tab_gs", J, U8)
        nc.vector.tensor_copy(tab_gw[:], tab_w[:].indirect(slots[:]))
        nc.vector.tensor_copy(tab_gs[:], tab_s[:].indirect(slots[:]))
        w1_words, w1_scales = quantise("w1", w1_bf, R)
        a_ps = ps.tile([P, J], F32, name="a_ps")
        nc.tensor.matmul_mx(out=a_ps[:], lhsT=w1_words[:].bitcast(FP8X4), lhsT_scale=w1_scales[:],
                            rhs=tab_gw[:].bitcast(FP4X4), rhs_scale=tab_gs[:], start=True, stop=True)
        h1 = sbuf("h1", J, on="lift_sb")
        nc.scalar.activation(h1[:], a_ps[:], ACT.Tanh)
        h1_sq = sbuf("h1_sq", J)
        nc.scalar.activation(h1_sq[:], h1[:], ACT.Square)

        dtab_gw = sbuf("dtab_gw", J, U16)
        dtab_gs = sbuf("dtab_gs", J, U8)
        nc.vector.tensor_copy(dtab_gs[:], dtab_s[:].indirect(slots[:]))
        nc.vector.tensor_copy(dtab_gw[:], dtab_w[:].indirect(slots[:]))
        ta_ps = ps.tile([P, J], F32, name="ta_ps")
        nc.tensor.matmul_mx(out=ta_ps[:], lhsT=w1_words[:].bitcast(FP8X4), lhsT_scale=w1_scales[:],
                            rhs=dtab_gw[:].bitcast(FP4X4), rhs_scale=dtab_gs[:], start=True, stop=True)

        dy_bf = interleave("dy_bf", dy_raw, M)
        wo_bf = interleave("wo_bf", wo_raw, R)

        h2 = shared.tile([P, J], F32, name="h2", offset=0)
        nc.vector.tensor_tensor(h2[:], h1[:], lifted[:], MULT)
        neg_ed = shared.tile([P, J], F32, name="neg_ed", offset=4 * J)
        nc.vector.scalar_tensor_tensor(neg_ed[:], h1_sq[:], 1.0, lifted[:], SUB, MULT)
        g = sbuf("g", M)
        nc.vector.tensor_copy(g[:], h2[:].indirect(picks[:]))

        th = sbuf("th", M, on="wo_raw")
        nc.scalar.activation(th[:], g[:], ACT.Tanh, scale=0.5)
        th_sq = sbuf("th_sq", M)
        nc.scalar.activation(th_sq[:], th[:], ACT.Square, scale=0.5)

        dy_words, dy_scales = quantise("dy", dy_bf, M)
        wo_words, wo_scales = quantise("wo", wo_bf, R)
        c0_ps = ps.tile([P, M], F32, name="c0_ps")
        nc.tensor.matmul_mx(out=c0_ps[:], lhsT=wo_words[:].bitcast(FP8X4), lhsT_scale=wo_scales[:],
                            rhs=dy_words[:].bitcast(FP8X4), rhs_scale=dy_scales[:], start=True, stop=True)
        c0 = sbuf("c0", M)
        nc.scalar.copy(c0[:], c0_ps[:])
        neg_2s = sbuf("neg_2s", M)
        nc.scalar.activation(neg_2s[:], th[:], ACT.Copy, bias=-1.0, scale=-1.0)
        neg_2w = sbuf("neg_2w", M)
        nc.scalar.activation(neg_2w[:], th_sq[:], ACT.Copy, bias=-0.5, scale=2.0)

        xh2 = sbuf("xh2", J, on="wo_bf")
        nc.vector.scalar_tensor_tensor(xh2[:], ta_ps[:], -1.0, neg_ed[:], MULT, MULT)
        neg_gw = sbuf("neg_gw", M, on="dy_bf")
        nc.vector.scalar_tensor_tensor(neg_gw[:], th_sq[:], 0.25, g[:], SUB, MULT)
        xc0 = sbuf("xc0", M)
        nc.vector.tensor_tensor(xc0[:], xh2[:].indirect(picks[:]), c0[:], MULT)
        neg_2f1 = sbuf("neg_2f1", M)
        nc.vector.scalar_tensor_tensor(neg_2f1[:], neg_gw[:], 2.0, neg_2s[:], MULT, ADD)
        neg_gwth = sbuf("neg_gwth", M)
        nc.vector.tensor_tensor(neg_gwth[:], neg_gw[:], th[:], MULT)
        nc.vector.tensor_tensor(placed_e1[:].indirect(picks[:]), neg_2f1[:], xc0[:], MULT)
        neg_f2 = sbuf("neg_f2", M, on="neg_2f1")
        nc.vector.tensor_tensor(neg_f2[:], neg_2w[:], neg_gwth[:], SUB)

        ident = sbuf("ident", P)
        make_identity(nc, ident[:])
        term_e1 = sbuf("term_e1", J)
        term_xe1 = sbuf("term_xe1", J)
        result = sbuf("result", J)
        nc.vector.scalar_tensor_tensor(term_e1[:], placed_e1[:], og_sb[:], h1[:], MULT, MULT)
        nc.vector.tensor_tensor(placed_xe1[:].indirect(picks[:]), neg_f2[:], xc0[:], MULT)

        turned = sbuf("turned", J)
        partial = [ps.tile([P, HALF], F32, name="partial", tag=bank) for bank in ("a_ps", "c0_ps")]
        blocks = [slice(b * P, (b + 1) * P) for b in range(J // P)]
        sums = [ps.tile([P, P], F32, name="sum%d" % b) for b in range(J // P)]
        for b, cols in enumerate(blocks):
            nc.tensor.matmul(sums[b][:], base_sb[:, cols], ident[:], start=True, stop=False, is_transpose=True)
        for b, cols in enumerate(blocks):
            nc.tensor.matmul(sums[b][:], term_e1[:, cols], ident[:], start=False, stop=True, is_transpose=True)
            nc.scalar.copy(turned[:, cols], sums[b][:])
        blocks_per_half = HALF // P
        for b, cols in enumerate(blocks):
            nc.tensor.transpose(partial[b // blocks_per_half][:, blocks[b % blocks_per_half]], turned[:, cols], ident[:])

        halves = [slice(h * HALF, (h + 1) * HALF) for h in range(J // HALF)]
        for cols in halves:
            nc.vector.scalar_tensor_tensor(term_xe1[:, cols], placed_xe1[:, cols], og_sb[:], neg_ed[:, cols], MULT, MULT)
        for cols, sum_ps, queue in zip(halves, partial, (nc.sync, nc.scalar)):
            nc.vector.tensor_tensor(result[:, cols], term_xe1[:, cols], sum_ps[:], ADD)
            queue.dma_start(out=out[:, cols], in_=result[:, cols])
